import numpy as np
import ml_dtypes


def mxq(x, axis, fmt="e4m3"):
    dtype, down = {"e4m3": (ml_dtypes.float8_e4m3fn, 7), "e5m2": (ml_dtypes.float8_e5m2, 14)}[fmt]
    v = np.moveaxis(np.asarray(x, np.float32).astype(ml_dtypes.bfloat16).astype(np.float64), axis, -1)
    blocks = v.reshape(v.shape[:-1] + (-1, 32))
    amax = np.abs(blocks).max(-1, keepdims=True)
    byte = np.maximum(np.where(amax > 0, np.frexp(amax)[1] - 1 + 127, 0) - down, 1)
    scale = np.exp2(byte - 127.0)
    codes = (blocks / scale).astype(np.float32).astype(dtype).astype(np.float64)
    return np.moveaxis((codes * scale).reshape(v.shape), -1, axis)


WIDE = False


def mx_kscale(k):
    if not WIDE:
        return np.ones(k)
    levels = np.array([10, -10, 5, -5, 0])
    if k % 512:
        return np.exp2(np.random.permutation(np.resize(levels, k // 32))).repeat(32)
    a = np.empty((k // 512, 16))
    for p in range(k // 512):
        a[p, :8] = np.random.permutation(np.resize(levels, 8))
        for g in range(8):
            far = levels[np.abs(levels - a[p, g]) >= 10]
            a[p, g + 8] = far[np.random.randint(len(far))]
    return np.exp2(a.ravel()).repeat(32)


def f64(x):
    return np.asarray(x).astype(np.float64)


def striped(idx):
    return np.tile(idx.reshape(-1, 16).T, (8, 1)).astype(np.uint16)


def unstriped(offs):
    return offs[:16].T.reshape(-1).astype(np.int64)


E2M1 = np.array([0.0, 0.5, 1.0, 1.5, 2.0, 3.0, 4.0, 6.0, -0.0, -0.5, -1.0, -1.5, -2.0, -3.0, -4.0, -6.0])


def pack_weight(w, fmt):
    k, n = w.shape
    w = f64(np.asarray(w, np.float32).astype(ml_dtypes.bfloat16)).reshape(k // 32, 32, n)
    amax = np.abs(w).max(1)
    if fmt == "e4m3":
        byte = np.frexp(amax)[1] - 1 + 127 - 7
    else:
        mant, ex = np.frexp(amax / 6.0)
        byte = np.where(mant > 0.5, ex, ex - 1) + 127
    byte = np.clip(np.where(amax > 0, byte, 1), 1, 254)
    scaled = (w * np.exp2(127.0 - byte)[:, None, :]).reshape(k, n).astype(np.float32)
    by_word = np.ascontiguousarray(scaled.reshape(k // 512, 128, 4, n).transpose(0, 1, 3, 2))
    if fmt == "e4m3":
        words = by_word.astype(ml_dtypes.float8_e4m3fn).view(np.uint8)
    else:
        c = by_word.astype(ml_dtypes.float4_e2m1fn).view(np.uint8) & 0xF
        words = (c[..., 0::2] | (c[..., 1::2] << 4)).reshape(k // 512, 128, 2 * n)
    return np.ascontiguousarray(words), np.ascontiguousarray(byte.astype(np.uint8).reshape(k // 512, 16, n))


def unpack_weight(words, scales, fmt):
    g, _, n = scales.shape
    words = np.ascontiguousarray(words).reshape(g, 128, n, -1)
    if fmt == "e4m3":
        vals = words.view(ml_dtypes.float8_e4m3fn).astype(np.float64)
    else:
        nib = np.empty((g, 128, n, 4), np.uint8)
        nib[..., 0::2] = words & 0xF
        nib[..., 1::2] = words >> 4
        vals = E2M1[nib]
    vals = vals * np.repeat(np.exp2(scales.astype(np.float64) - 127.0), 8, axis=1)[..., None]
    return vals.transpose(0, 1, 3, 2).reshape(g * 512, n)


def relu(v):
    return np.maximum(v, 0.0)


K, T, E, C, N = 1024, 1024, 12, 256, 256
TOP = 3


def by_expert(wq, xq):
    return np.concatenate([wq[e].T @ xq[:, e * C:(e + 1) * C] for e in range(E)], axis=1)


def setup_inputs():
    n = np.random.standard_normal
    s = mx_kscale(K)[:, None]
    deal = np.repeat(np.arange(E), C).reshape(TOP, T)[:, np.random.permutation(T)]
    deal = np.take_along_axis(deal, np.argsort(np.random.rand(TOP, T), axis=0), axis=0)
    for _ in range(8):
        s_, t_ = np.random.permutation(T).reshape(2, -1); r = np.random.randint(TOP, size=T // 2); x, y = deal[r, s_].copy(), deal[r, t_].copy()
        ok = ~((deal[:, s_] == y).any(0) | (deal[:, t_] == x).any(0)); deal[r[ok], s_[ok]] = y[ok]; deal[r[ok], t_[ok]] = x[ok]
    order = np.lexsort((np.random.rand(TOP * T), deal.reshape(-1)))
    slot_token = order % T; pos = np.empty(TOP * T, np.int64); pos[order] = np.arange(TOP * T); pos = pos.reshape(TOP, T)
    g = np.random.uniform(0.5, 1.5, (TOP, T)); g = g / g.sum(0)
    w = [pack_weight(m, "e2m1") for m in n((E, K, N)) / np.sqrt(K) / s[None]]
    return {
        "xT": (n((K, T)) * s).astype(np.float32),
        "w_words": np.stack([m[0] for m in w]),
        "w_scales": np.stack([m[1] for m in w]),
        "b": (0.3 * n((N, E))).astype(np.float32),
        "gate": np.stack([np.tile(r, (N, 1)) for r in g]).astype(np.float32),
        "offs": striped(slot_token),
        "pos1": striped(pos[0]),
        "pos2": striped(pos[1]),
        "pos3": striped(pos[2]),
    }


def reference(xT, w_words, w_scales, b, gate, offs, pos1, pos2, pos3):
    idx = unstriped(offs)
    w = np.stack([unpack_weight(w_words[e], w_scales[e], "e2m1") for e in range(E)])
    xq = mxq(f64(xT)[:, idx], 0, "e4m3")
    y = by_expert(w, xq)
    y = relu(y + np.repeat(f64(b), C, axis=1))
    return sum(f64(gate[r]) * y[:, unstriped(p)] for r, p in enumerate((pos1, pos2, pos3)))

@@ -1,0 +1,165 @@
+from contextlib import ExitStack
+
+import concourse.mybir as mybir
+
+K, T, E, C, N = 1024, 1024, 12, 256, 256
+TOP = 3
+FLOPS = 2 * K * N * E * C
+
+F32 = mybir.dt.float32
+BF16 = mybir.dt.bfloat16
+I32 = mybir.dt.int32
+U32 = mybir.dt.uint32
+U16 = mybir.dt.uint16
+U8 = mybir.dt.uint8
+FP8X4 = mybir.dt.float8_e4m3fn_x4
+FP4X4 = mybir.dt.float4_e2m1fn_x4
+MULT, ADD = mybir.AluOpType.mult, mybir.AluOpType.add
+COPY = mybir.ActivationFunctionType.Copy
+RELU = mybir.ActivationFunctionType.Relu
+
+P = 128
+PASSES = K // 512
+SLOTS = E * C
+HALVES = N // P
+SHIFT = 4
+CHUNKS = (((0, 512), (512, 256), (768, 256)), ((0, 512), (512, 512)))
+ON_SCALAR = ((192, 96, 96), (512, 512))
+
+
+def tile_moe_tk_lin_relu_kernel(tc, xT, w_words, w_scales, b, gate, offs, pos1, pos2, pos3, out):
+    nc = tc.nc
+    with ExitStack() as ctx:
+        lists = ctx.enter_context(tc.tile_pool(name="lists", bufs=1))
+        keep = ctx.enter_context(tc.tile_pool(name="keep", bufs=1))
+        work = ctx.enter_context(tc.tile_pool(name="work", bufs=2))
+        psum = ctx.enter_context(tc.psum_pool(name="psum", bufs=8))
+
+        offs_t = lists.tile([P, SLOTS // 16], U16, name="offs_t")
+        pos_t = [lists.tile([P, T // 16], U16, name=f"pos{r}_t") for r in range(TOP)]
+
+        raw = [[keep.tile([P, 4, n], F32, name=f"raw{a}_{lo}") for lo, n in CHUNKS[a]] for a in range(PASSES)]
+        grouped = [[keep.tile([P, n, 4], BF16, align_bytes=64, name=f"grouped{a}_{lo}") for lo, n in CHUNKS[a]] for a in range(PASSES)]
+        codes = [keep.tile([P, T], U32, align_bytes=64, name=f"codes{a}") for a in range(PASSES)]
+        scales = keep.tile([P, T], U8, align_bytes=64, name="scales")
+        g_codes = [keep.tile([P, SLOTS], U32, align_bytes=64, name=f"g_codes{a}") for a in range(PASSES)]
+        g_scales = keep.tile([P, SLOTS], U8, align_bytes=64, name="g_scales")
+        g_scales1 = keep.tile([P, SLOTS], U8, align_bytes=64, name="g_scales1")
+        w_t = keep.tile([P, E * PASSES, 2 * N], U8, align_bytes=64, name="w_t")
+        ws_t = keep.tile([P, E * PASSES, N], U8, align_bytes=64, name="ws_t")
+        b_t = keep.tile([P, HALVES, E], F32, name="b_t")
+        gate_t = keep.tile([P, TOP, T], F32, name="gate_t")
+        y = [keep.tile([P, SLOTS], F32, name=f"y{h}") for h in range(HALVES)]
+
+        nc.gpsimd.memset(scales[:], 0)
+        nc.gpsimd.memset(ws_t[:].rearrange("p g n -> p (g n)").bitcast(I32), 0)
+        nc.gpsimd.memset(g_scales1[:].bitcast(I32), 0)
+
+        def load_x(a, c):
+            lo, n = CHUNKS[a][c]
+            src = xT[512 * a : 512 * (a + 1), lo : lo + n].rearrange("(p j) w -> p j w", j=4)
+            nc.sync.dma_start(out=raw[a][c][:], in_=src)
+
+        load_x(0, 0)
+        load_x(0, 1)
+        load_x(0, 2)
+        nc.sync.dma_start(offs_t[:], offs)
+        load_x(1, 0)
+        load_x(1, 1)
+        w_src = w_words.bitcast(I32).rearrange("e a p n -> p (e a) n")
+        ws_src = w_scales.bitcast(I32)
+        for q in range(4):
+            nc.sync.dma_start(
+                out=ws_t[32 * q : 32 * q + 4].bitcast(I32),
+                in_=ws_src[:, :, 4 * q : 4 * q + 4, :].rearrange("e a r n -> r (e a) n"),
+            )
+        for s in range(3):
+            g = slice(8 * s, 8 * s + 8)
+            nc.sync.dma_start(out=w_t[:, g, :].bitcast(I32), in_=w_src[:, g, :])
+        nc.sync.dma_start(out=b_t[:], in_=b.rearrange("(h p) e -> p h e", p=P))
+        for r, src in enumerate((pos1, pos2, pos3)):
+            nc.sync.dma_start(pos_t[r][:], src)
+        for r in range(TOP):
+            nc.sync.dma_start(out=gate_t[:, r, :], in_=gate[r, 0:P, :])
+
+        def cast(engine, a, c, lo, hi):
+            dst = grouped[a][c][:, lo:hi, :]
+            src = raw[a][c][:, :, lo:hi].rearrange("p j w -> p w j")
+            if engine == "v":
+                nc.vector.tensor_copy(out=dst, in_=src)
+            else:
+                nc.scalar.activation(dst, src, COPY)
+
+        def quantize(a, c):
+            lo, n = CHUNKS[a][c]
+            nc.vector.quantize_mx(
+                out=codes[a][:, lo : lo + n].bitcast(FP8X4),
+                scales=scales[SHIFT * a : P, lo : lo + n],
+                in_=grouped[a][c][:].rearrange("p w j -> p (w j)"),
+            )
+
+        for a in range(PASSES):
+            for c in range(len(CHUNKS[a])):
+                n, cut = CHUNKS[a][c][1], ON_SCALAR[a][c]
+                cast("s", a, c, 0, cut)
+                if cut < n:
+                    cast("v", a, c, cut, n)
+                if a == 0:
+                    quantize(a, c)
+
+        def gather_codes(a, lo, hi):
+            nc.vector.tensor_copy(g_codes[a][:, lo:hi], codes[a][:].indirect(offs_t[:, lo // 16 : hi // 16]))
+
+        def gather_scales(lo, hi):
+            nc.vector.tensor_copy(g_scales[:, lo:hi], scales[:].indirect(offs_t[:, lo // 16 : hi // 16]))
+            nc.sync.dma_start(out=g_scales1[0 : P - SHIFT, lo:hi].bitcast(I32), in_=g_scales[SHIFT:P, lo:hi].bitcast(I32))
+
+        def expert(e):
+            ps = psum.tile([P, HALVES * C], F32, name="ps")
+            for h in range(HALVES):
+                for s in range(2):
+                    slots = slice(e * C + s * P, e * C + (s + 1) * P)
+                    o = h * C + s * P
+                    for a in range(PASSES):
+                        g = e * PASSES + a
+                        plane = (g_scales, g_scales1)[a]
+                        nc.tensor.matmul_mx(
+                            out=ps[:, o : o + P],
+                            lhsT=w_t[:, g, 2 * P * h : 2 * P * (h + 1)].bitcast(FP4X4),
+                            lhsT_scale=ws_t[:, g, P * h : P * (h + 1)],
+                            rhs=g_codes[a][:, slots].bitcast(FP8X4),
+                            rhs_scale=plane[:, slots],
+                            start=(a == 0),
+                            stop=(a == PASSES - 1),
+                        )
+                nc.scalar.activation(
+                    y[h][:, e * C : (e + 1) * C], ps[:, h * C : (h + 1) * C], RELU, bias=b_t[:, h, e : e + 1]
+                )
+
+        for lo in range(0, SLOTS, 768):
+            gather_codes(0, lo, lo + 768)
+        for c in range(2):
+            quantize(1, c)
+        gather_scales(0, 768)
+        gather_scales(768, 1536)
+        for lo, n, ahead in ((0, 768, 1536), (768, 768, 2304), (1536, 768, None), (2304, 512, None), (2816, 256, None)):
+            gather_codes(1, lo, lo + n)
+            if ahead is not None:
+                gather_scales(ahead, ahead + 768)
+            for e in range(lo // C, (lo + n) // C):
+                expert(e)
+
+        def combine(h, lo, hi):
+            prods = []
+            for r in range(TOP):
+                prod = work.tile([P, hi - lo], F32, name=f"prod{r}_{hi - lo}")
+                nc.vector.tensor_tensor(prod[:], y[h][:].indirect(pos_t[r][:, lo // 16 : hi // 16]), gate_t[:, r, lo:hi], MULT)
+                prods.append(prod)
+                if r == 1:
+                    nc.vector.tensor_tensor(prods[0][:], prods[0][:], prods[1][:], ADD)
+            nc.vector.tensor_tensor(prods[2][:], prods[0][:], prods[2][:], ADD)
+            nc.sync.dma_start(out=out[h * P : (h + 1) * P, lo:hi], in_=prods[2][:])
+
+        combine(0, 0, T)
+        combine(1, 0, T // 2)
+        combine(1, T // 2, T)

@@ -14,7 +14,7 @@ U16 = mybir.dt.uint16
 U8 = mybir.dt.uint8
 FP8X4 = mybir.dt.float8_e4m3fn_x4
 FP4X4 = mybir.dt.float4_e2m1fn_x4
-MULT, ADD = mybir.AluOpType.mult, mybir.AluOpType.add
+MULT, ADD, MAX = mybir.AluOpType.mult, mybir.AluOpType.add, mybir.AluOpType.max
 COPY = mybir.ActivationFunctionType.Copy
 RELU = mybir.ActivationFunctionType.Relu
 
@@ -23,8 +23,10 @@ PASSES = K // 512
 SLOTS = E * C
 HALVES = N // P
 SHIFT = 4
+CUT = 640
+PIECE = 768
 CHUNKS = (((0, 512), (512, 256), (768, 256)), ((0, 512), (512, 512)))
-ON_SCALAR = ((192, 96, 96), (512, 512))
+ON_SCALAR = ((192, 192, 96), (512, 512))
 
 
 def tile_moe_tk_lin_relu_kernel(tc, xT, w_words, w_scales, b, gate, offs, pos1, pos2, pos3, out):
@@ -32,6 +34,8 @@ def tile_moe_tk_lin_relu_kernel(tc, xT, w_words, w_scales, b, gate, offs, pos1, 
     with ExitStack() as ctx:
         lists = ctx.enter_context(tc.tile_pool(name="lists", bufs=1))
         keep = ctx.enter_context(tc.tile_pool(name="keep", bufs=1))
+        late = ctx.enter_context(tc.tile_pool(name="late", bufs=1))
+        gathered = [ctx.enter_context(tc.tile_pool(name=f"gathered{a}", bufs=3 + a)) for a in range(PASSES)]
         work = ctx.enter_context(tc.tile_pool(name="work", bufs=2))
         psum = ctx.enter_context(tc.psum_pool(name="psum", bufs=8))
 
@@ -39,21 +43,24 @@ def tile_moe_tk_lin_relu_kernel(tc, xT, w_words, w_scales, b, gate, offs, pos1, 
         pos_t = [lists.tile([P, T // 16], U16, name=f"pos{r}_t") for r in range(TOP)]
 
         raw = [[keep.tile([P, 4, n], F32, name=f"raw{a}_{lo}") for lo, n in CHUNKS[a]] for a in range(PASSES)]
-        grouped = [[keep.tile([P, n, 4], BF16, align_bytes=64, name=f"grouped{a}_{lo}") for lo, n in CHUNKS[a]] for a in range(PASSES)]
+        grouped = [
+            [keep.tile([P, n, 4], BF16, align_bytes=64, name=f"grouped0_{lo}") for lo, n in CHUNKS[0]],
+            [keep.tile([P, n, 4], BF16, align_bytes=64, name=f"grouped1_{lo}") for lo, n in CHUNKS[1]],
+        ]
         codes = [keep.tile([P, T], U32, align_bytes=64, name=f"codes{a}") for a in range(PASSES)]
-        scales = keep.tile([P, T], U8, align_bytes=64, name="scales")
-        g_codes = [keep.tile([P, SLOTS], U32, align_bytes=64, name=f"g_codes{a}") for a in range(PASSES)]
-        g_scales = keep.tile([P, SLOTS], U8, align_bytes=64, name="g_scales")
-        g_scales1 = keep.tile([P, SLOTS], U8, align_bytes=64, name="g_scales1")
+        scales = late.tile([P, T], U8, align_bytes=64, name="scales")
+        g_codes = [{}, {}]
+        g_scales = [keep.tile([P, PIECE], U8, align_bytes=64, name=f"g_scales_{c}") for c in range(SLOTS // PIECE)]
+        g_scales1 = [keep.tile([P, PIECE], U8, align_bytes=64, name=f"g_scales1_{c}") for c in range(SLOTS // PIECE)]
         w_t = keep.tile([P, E * PASSES, 2 * N], U8, align_bytes=64, name="w_t")
         ws_t = keep.tile([P, E * PASSES, N], U8, align_bytes=64, name="ws_t")
         b_t = keep.tile([P, HALVES, E], F32, name="b_t")
-        gate_t = keep.tile([P, TOP, T], F32, name="gate_t")
         y = [keep.tile([P, SLOTS], F32, name=f"y{h}") for h in range(HALVES)]
 
         nc.gpsimd.memset(scales[:], 0)
         nc.gpsimd.memset(ws_t[:].rearrange("p g n -> p (g n)").bitcast(I32), 0)
-        nc.gpsimd.memset(g_scales1[:].bitcast(I32), 0)
+        for c in range(SLOTS // PIECE):
+            nc.gpsimd.memset(g_scales1[c][:].bitcast(I32), 0)
 
         def load_x(a, c):
             lo, n = CHUNKS[a][c]
@@ -79,8 +86,6 @@ def tile_moe_tk_lin_relu_kernel(tc, xT, w_words, w_scales, b, gate, offs, pos1, 
         nc.sync.dma_start(out=b_t[:], in_=b.rearrange("(h p) e -> p h e", p=P))
         for r, src in enumerate((pos1, pos2, pos3)):
             nc.sync.dma_start(pos_t[r][:], src)
-        for r in range(TOP):
-            nc.sync.dma_start(out=gate_t[:, r, :], in_=gate[r, 0:P, :])
 
         def cast(engine, a, c, lo, hi):
             dst = grouped[a][c][:, lo:hi, :]
@@ -108,58 +113,97 @@ def tile_moe_tk_lin_relu_kernel(tc, xT, w_words, w_scales, b, gate, offs, pos1, 
                     quantize(a, c)
 
         def gather_codes(a, lo, hi):
-            nc.vector.tensor_copy(g_codes[a][:, lo:hi], codes[a][:].indirect(offs_t[:, lo // 16 : hi // 16]))
+            c, o = divmod(lo, PIECE)
+            if o == 0:
+                if (a, c) == (0, 3):
+                    g_codes[a][c] = late.tile([P, PIECE], U32, align_bytes=64, name="scales")
+                else:
+                    g_codes[a][c] = gathered[a].tile([P, PIECE], U32, align_bytes=64, name=f"g_codes{a}")
+            nc.vector.tensor_copy(g_codes[a][c][:, o : o + hi - lo], codes[a][:].indirect(offs_t[:, lo // 16 : hi // 16]))
 
-        def gather_scales(lo, hi):
-            nc.vector.tensor_copy(g_scales[:, lo:hi], scales[:].indirect(offs_t[:, lo // 16 : hi // 16]))
-            nc.sync.dma_start(out=g_scales1[0 : P - SHIFT, lo:hi].bitcast(I32), in_=g_scales[SHIFT:P, lo:hi].bitcast(I32))
+        def gather_scales(c):
+            nc.vector.tensor_copy(g_scales[c][:], scales[:].indirect(offs_t[:, PIECE * c // 16 : PIECE * (c + 1) // 16]))
+            nc.sync.dma_start(out=g_scales1[c][0 : P - SHIFT, :].bitcast(I32), in_=g_scales[c][SHIFT:P, :].bitcast(I32))
+
+        def one_pass(ps, o, e, h, s, a):
+            g = e * PASSES + a
+            c, at = divmod(e * C + s * P, PIECE)
+            nc.tensor.matmul_mx(
+                out=ps[:, o : o + P],
+                lhsT=w_t[:, g, 2 * P * h : 2 * P * (h + 1)].bitcast(FP4X4),
+                lhsT_scale=ws_t[:, g, P * h : P * (h + 1)],
+                rhs=g_codes[a][c][:, at : at + P].bitcast(FP8X4),
+                rhs_scale=(g_scales, g_scales1)[a][c][:, at : at + P],
+                start=(a == 1),
+                stop=(a == 0),
+            )
 
         def expert(e):
             ps = psum.tile([P, HALVES * C], F32, name="ps")
             for h in range(HALVES):
                 for s in range(2):
-                    slots = slice(e * C + s * P, e * C + (s + 1) * P)
-                    o = h * C + s * P
-                    for a in range(PASSES):
-                        g = e * PASSES + a
-                        plane = (g_scales, g_scales1)[a]
-                        nc.tensor.matmul_mx(
-                            out=ps[:, o : o + P],
-                            lhsT=w_t[:, g, 2 * P * h : 2 * P * (h + 1)].bitcast(FP4X4),
-                            lhsT_scale=ws_t[:, g, P * h : P * (h + 1)],
-                            rhs=g_codes[a][:, slots].bitcast(FP8X4),
-                            rhs_scale=plane[:, slots],
-                            start=(a == 0),
-                            stop=(a == PASSES - 1),
-                        )
+                    for a in (1, 0):
+                        one_pass(ps, h * C + s * P, e, h, s, a)
                 nc.scalar.activation(
                     y[h][:, e * C : (e + 1) * C], ps[:, h * C : (h + 1) * C], RELU, bias=b_t[:, h, e : e + 1]
                 )
 
-        for lo in range(0, SLOTS, 768):
-            gather_codes(0, lo, lo + 768)
-        for c in range(2):
+        def words(a, lo, n):
+            gather_codes(a, lo, lo + n)
+
+        for c in range(3):
+            words(0, PIECE * c, PIECE)
+        for c in range(len(CHUNKS[1])):
             quantize(1, c)
-        gather_scales(0, 768)
-        gather_scales(768, 1536)
-        for lo, n, ahead in ((0, 768, 1536), (768, 768, 2304), (1536, 768, None), (2304, 512, None), (2816, 256, None)):
-            gather_codes(1, lo, lo + n)
-            if ahead is not None:
-                gather_scales(ahead, ahead + 768)
-            for e in range(lo // C, (lo + n) // C):
-                expert(e)
+        gather_scales(0)
+        gather_scales(1)
+        words(1, 0, PIECE)
+        for e in range(3):
+            expert(e)
+        gather_scales(2)
+        words(1, PIECE, PIECE)
+        for e in range(3, 6):
+            expert(e)
+        gather_scales(3)
+        words(1, 2 * PIECE, PIECE)
+        for e in range(6, 9):
+            expert(e)
+        words(0, 3 * PIECE, PIECE)
+        for e in range(9, E):
+            words(1, e * C, C)
+            expert(e)
 
-        def combine(h, lo, hi):
-            prods = []
-            for r in range(TOP):
-                prod = work.tile([P, hi - lo], F32, name=f"prod{r}_{hi - lo}")
-                nc.vector.tensor_tensor(prod[:], y[h][:].indirect(pos_t[r][:, lo // 16 : hi // 16]), gate_t[:, r, lo:hi], MULT)
-                prods.append(prod)
-                if r == 1:
-                    nc.vector.tensor_tensor(prods[0][:], prods[0][:], prods[1][:], ADD)
-            nc.vector.tensor_tensor(prods[2][:], prods[0][:], prods[2][:], ADD)
-            nc.sync.dma_start(out=out[h * P : (h + 1) * P, lo:hi], in_=prods[2][:])
+        gate_t = []
+        for r, a in enumerate((1, 1, 0)):
+            gate_t.append(gathered[a].tile([P, T], F32, align_bytes=64, name=f"g_codes{a}"))
+            nc.sync.dma_start(out=gate_t[r][:], in_=gate[r, 0:P, :])
 
-        combine(0, 0, T)
-        combine(1, 0, T // 2)
-        combine(1, T // 2, T)
+        def product(h, r, lo, hi):
+            prod = work.tile([P, hi - lo], F32, name=f"prod{r}_{hi - lo}")
+            nc.vector.tensor_tensor(prod[:], y[h][:].indirect(pos_t[r][:, lo // 16 : hi // 16]), gate_t[r][:, lo:hi], MULT)
+            return prod
+
+        def add(into, other):
+            nc.vector.tensor_tensor(into[:], into[:], other[:], ADD)
+
+        def store(h, lo, hi, total):
+            nc.sync.dma_start(out=out[h * P : (h + 1) * P, lo:hi], in_=total[:])
+
+        a0 = product(0, 0, 0, T)
+        a1 = product(0, 1, 0, T)
+        a2 = product(0, 2, 0, T)
+        add(a0, a1)
+        b0 = product(1, 0, 0, CUT)
+        add(a0, a2)
+        store(0, 0, T, a0)
+        b1 = product(1, 1, 0, CUT)
+        b2 = product(1, 2, 0, CUT)
+        add(b0, b1)
+        c0 = product(1, 0, CUT, T)
+        add(b0, b2)
+        store(1, 0, CUT, b0)
+        c1 = product(1, 1, CUT, T)
+        c2 = product(1, 2, CUT, T)
+        add(c0, c1)
+        add(c0, c2)
+        store(1, CUT, T, c0)

@@ -88,8 +88,8 @@ def tile_moe_tk_lin_relu_kernel(tc, xT, w_words, w_scales, b, gate, offs, pos1, 
             nc.sync.dma_start(pos_t[r][:], src)
 
         def cast(engine, a, c, lo, hi):
-            dst = grouped[a][c][:, lo:hi, :]
-            src = raw[a][c][:, :, lo:hi].rearrange("p j w -> p w j")
+            dst = grouped[a][c][:, lo:hi, :].rearrange("p (c i) j -> p c j i", i=4)
+            src = raw[a][c][:, :, lo:hi].rearrange("p j (c i) -> p c j i", i=4)
             if engine == "v":
                 nc.vector.tensor_copy(out=dst, in_=src)
             else:
@@ -138,15 +138,16 @@ def tile_moe_tk_lin_relu_kernel(tc, xT, w_words, w_scales, b, gate, offs, pos1, 
                 stop=(a == 0),
             )
 
+        def half(e, h):
+            ps = psum.tile([P, C], F32, name="ps")
+            for s in range(2):
+                for a in (1, 0):
+                    one_pass(ps, s * P, e, h, s, a)
+            nc.scalar.activation(y[h][:, e * C : (e + 1) * C], ps[:], RELU, bias=b_t[:, h, e : e + 1])
+
         def expert(e):
-            ps = psum.tile([P, HALVES * C], F32, name="ps")
             for h in range(HALVES):
-                for s in range(2):
-                    for a in (1, 0):
-                        one_pass(ps, h * C + s * P, e, h, s, a)
-                nc.scalar.activation(
-                    y[h][:, e * C : (e + 1) * C], ps[:, h * C : (h + 1) * C], RELU, bias=b_t[:, h, e : e + 1]
-                )
+                half(e, h)
 
         def words(a, lo, n):
             gather_codes(a, lo, lo + n)
@@ -167,11 +168,13 @@ def tile_moe_tk_lin_relu_kernel(tc, xT, w_words, w_scales, b, gate, offs, pos1, 
         gather_scales(3)
         words(1, 2 * PIECE, PIECE)
         for e in range(6, 9):
-            expert(e)
+            half(e, 0)
         words(0, 3 * PIECE, PIECE)
         for e in range(9, E):
             words(1, e * C, C)
-            expert(e)
+            half(e, 0)
+        for e in range(6, E):
+            half(e, 1)
 
         gate_t = []
         for r, a in enumerate((1, 1, 0)):

@@ -23,7 +23,7 @@ PASSES = K // 512
 SLOTS = E * C
 HALVES = N // P
 SHIFT = 4
-CUT = 640
+CUT = 768
 PIECE = 768
 CHUNKS = (((0, 512), (512, 256), (768, 256)), ((0, 512), (512, 512)))
 ON_SCALAR = ((192, 192, 96), (512, 512))
@@ -68,9 +68,9 @@ def tile_moe_tk_lin_relu_kernel(tc, xT, w_words, w_scales, b, gate, offs, pos1, 
             nc.sync.dma_start(out=raw[a][c][:], in_=src)
 
         load_x(0, 0)
+        nc.sync.dma_start(offs_t[:], offs)
         load_x(0, 1)
         load_x(0, 2)
-        nc.sync.dma_start(offs_t[:], offs)
         load_x(1, 0)
         load_x(1, 1)
         w_src = w_words.bitcast(I32).rearrange("e a p n -> p (e a) n")
@@ -125,7 +125,7 @@ def tile_moe_tk_lin_relu_kernel(tc, xT, w_words, w_scales, b, gate, offs, pos1, 
             nc.vector.tensor_copy(g_scales[c][:], scales[:].indirect(offs_t[:, PIECE * c // 16 : PIECE * (c + 1) // 16]))
             nc.sync.dma_start(out=g_scales1[c][0 : P - SHIFT, :].bitcast(I32), in_=g_scales[c][SHIFT:P, :].bitcast(I32))
 
-        def one_pass(ps, o, e, h, s, a):
+        def one_pass(ps, o, e, h, s, a, first=1):
             g = e * PASSES + a
             c, at = divmod(e * C + s * P, PIECE)
             nc.tensor.matmul_mx(
@@ -134,8 +134,8 @@ def tile_moe_tk_lin_relu_kernel(tc, xT, w_words, w_scales, b, gate, offs, pos1, 
                 lhsT_scale=ws_t[:, g, P * h : P * (h + 1)],
                 rhs=g_codes[a][c][:, at : at + P].bitcast(FP8X4),
                 rhs_scale=(g_scales, g_scales1)[a][c][:, at : at + P],
-                start=(a == 1),
-                stop=(a == 0),
+                start=(a == first),
+                stop=(a != first),
             )
 
         def half(e, h):
@@ -170,9 +170,19 @@ def tile_moe_tk_lin_relu_kernel(tc, xT, w_words, w_scales, b, gate, offs, pos1, 
         for e in range(6, 9):
             half(e, 0)
         words(0, 3 * PIECE, PIECE)
-        for e in range(9, E):
+        ends = []
+        for s in range(2):
+            ps = psum.tile([P, C], F32, name="ps")
+            one_pass(ps, 0, E - 1, 0, s, 0, first=0)
+            ends.append(ps)
+        for e in range(9, E - 1):
             words(1, e * C, C)
             half(e, 0)
+        words(1, (E - 1) * C, C)
+        for s in range(2):
+            one_pass(ends[s], 0, E - 1, 0, s, 1, first=0)
+            at = (E - 1) * C + s * P
+            nc.scalar.activation(y[0][:, at : at + P], ends[s][:, 0:P], RELU, bias=b_t[:, 0, E - 1 : E])
         for e in range(6, E):
             half(e, 1)
 

@@ -23,10 +23,10 @@ PASSES = K // 512
 SLOTS = E * C
 HALVES = N // P
 SHIFT = 4
-CUT = 768
+CUT = 896
 PIECE = 768
 CHUNKS = (((0, 512), (512, 256), (768, 256)), ((0, 512), (512, 512)))
-ON_SCALAR = ((192, 192, 96), (512, 512))
+ON_SCALAR = ((192, 192, 96), (512, 416))
 
 
 def tile_moe_tk_lin_relu_kernel(tc, xT, w_words, w_scales, b, gate, offs, pos1, pos2, pos3, out):

from contextlib import ExitStack

import concourse.mybir as mybir

K, T, E, C, N = 1024, 1024, 12, 256, 256
TOP = 3
FLOPS = 2 * K * N * E * C

F32 = mybir.dt.float32
BF16 = mybir.dt.bfloat16
I32 = mybir.dt.int32
U32 = mybir.dt.uint32
U16 = mybir.dt.uint16
U8 = mybir.dt.uint8
FP8X4 = mybir.dt.float8_e4m3fn_x4
FP4X4 = mybir.dt.float4_e2m1fn_x4
MULT, ADD, MAX = mybir.AluOpType.mult, mybir.AluOpType.add, mybir.AluOpType.max
COPY = mybir.ActivationFunctionType.Copy
RELU = mybir.ActivationFunctionType.Relu

P = 128
PASSES = K // 512
SLOTS = E * C
HALVES = N // P
SHIFT = 4
CUT = 896
PIECE = 768
CHUNKS = (((0, 512), (512, 256), (768, 256)), ((0, 512), (512, 512)))
ON_SCALAR = ((192, 192, 96), (512, 416))


def tile_moe_tk_lin_relu_kernel(tc, xT, w_words, w_scales, b, gate, offs, pos1, pos2, pos3, out):
    nc = tc.nc
    with ExitStack() as ctx:
        lists = ctx.enter_context(tc.tile_pool(name="lists", bufs=1))
        keep = ctx.enter_context(tc.tile_pool(name="keep", bufs=1))
        late = ctx.enter_context(tc.tile_pool(name="late", bufs=1))
        gathered = [ctx.enter_context(tc.tile_pool(name=f"gathered{a}", bufs=3 + a)) for a in range(PASSES)]
        work = ctx.enter_context(tc.tile_pool(name="work", bufs=2))
        psum = ctx.enter_context(tc.psum_pool(name="psum", bufs=8))

        offs_t = lists.tile([P, SLOTS // 16], U16, name="offs_t")
        pos_t = [lists.tile([P, T // 16], U16, name=f"pos{r}_t") for r in range(TOP)]

        raw = [[keep.tile([P, 4, n], F32, name=f"raw{a}_{lo}") for lo, n in CHUNKS[a]] for a in range(PASSES)]
        grouped = [
            [keep.tile([P, n, 4], BF16, align_bytes=64, name=f"grouped0_{lo}") for lo, n in CHUNKS[0]],
            [keep.tile([P, n, 4], BF16, align_bytes=64, name=f"grouped1_{lo}") for lo, n in CHUNKS[1]],
        ]
        codes = [keep.tile([P, T], U32, align_bytes=64, name=f"codes{a}") for a in range(PASSES)]
        scales = late.tile([P, T], U8, align_bytes=64, name="scales")
        g_codes = [{}, {}]
        g_scales = [keep.tile([P, PIECE], U8, align_bytes=64, name=f"g_scales_{c}") for c in range(SLOTS // PIECE)]
        g_scales1 = [keep.tile([P, PIECE], U8, align_bytes=64, name=f"g_scales1_{c}") for c in range(SLOTS // PIECE)]
        w_t = keep.tile([P, E * PASSES, 2 * N], U8, align_bytes=64, name="w_t")
        ws_t = keep.tile([P, E * PASSES, N], U8, align_bytes=64, name="ws_t")
        b_t = keep.tile([P, HALVES, E], F32, name="b_t")
        y = [keep.tile([P, SLOTS], F32, name=f"y{h}") for h in range(HALVES)]

        nc.gpsimd.memset(scales[:], 0)
        nc.gpsimd.memset(ws_t[:].rearrange("p g n -> p (g n)").bitcast(I32), 0)
        for c in range(SLOTS // PIECE):
            nc.gpsimd.memset(g_scales1[c][:].bitcast(I32), 0)

        def load_x(a, c):
            lo, n = CHUNKS[a][c]
            src = xT[512 * a : 512 * (a + 1), lo : lo + n].rearrange("(p j) w -> p j w", j=4)
            nc.sync.dma_start(out=raw[a][c][:], in_=src)

        load_x(0, 0)
        nc.sync.dma_start(offs_t[:], offs)
        load_x(0, 1)
        load_x(0, 2)
        load_x(1, 0)
        load_x(1, 1)
        w_src = w_words.bitcast(I32).rearrange("e a p n -> p (e a) n")
        ws_src = w_scales.bitcast(I32)
        for q in range(4):
            nc.sync.dma_start(
                out=ws_t[32 * q : 32 * q + 4].bitcast(I32),
                in_=ws_src[:, :, 4 * q : 4 * q + 4, :].rearrange("e a r n -> r (e a) n"),
            )
        for s in range(3):
            g = slice(8 * s, 8 * s + 8)
            nc.sync.dma_start(out=w_t[:, g, :].bitcast(I32), in_=w_src[:, g, :])
        nc.sync.dma_start(out=b_t[:], in_=b.rearrange("(h p) e -> p h e", p=P))
        for r, src in enumerate((pos1, pos2, pos3)):
            nc.sync.dma_start(pos_t[r][:], src)

        def cast(engine, a, c, lo, hi):
            dst = grouped[a][c][:, lo:hi, :].rearrange("p (c i) j -> p c j i", i=4)
            src = raw[a][c][:, :, lo:hi].rearrange("p j (c i) -> p c j i", i=4)
            if engine == "v":
                nc.vector.tensor_copy(out=dst, in_=src)
            else:
                nc.scalar.activation(dst, src, COPY)

        def quantize(a, c):
            lo, n = CHUNKS[a][c]
            nc.vector.quantize_mx(
                out=codes[a][:, lo : lo + n].bitcast(FP8X4),
                scales=scales[SHIFT * a : P, lo : lo + n],
                in_=grouped[a][c][:].rearrange("p w j -> p (w j)"),
            )

        for a in range(PASSES):
            for c in range(len(CHUNKS[a])):
                n, cut = CHUNKS[a][c][1], ON_SCALAR[a][c]
                cast("s", a, c, 0, cut)
                if cut < n:
                    cast("v", a, c, cut, n)
                if a == 0:
                    quantize(a, c)

        def gather_codes(a, lo, hi):
            c, o = divmod(lo, PIECE)
            if o == 0:
                if (a, c) == (0, 3):
                    g_codes[a][c] = late.tile([P, PIECE], U32, align_bytes=64, name="scales")
                else:
                    g_codes[a][c] = gathered[a].tile([P, PIECE], U32, align_bytes=64, name=f"g_codes{a}")
            nc.vector.tensor_copy(g_codes[a][c][:, o : o + hi - lo], codes[a][:].indirect(offs_t[:, lo // 16 : hi // 16]))

        def gather_scales(c):
            nc.vector.tensor_copy(g_scales[c][:], scales[:].indirect(offs_t[:, PIECE * c // 16 : PIECE * (c + 1) // 16]))
            nc.sync.dma_start(out=g_scales1[c][0 : P - SHIFT, :].bitcast(I32), in_=g_scales[c][SHIFT:P, :].bitcast(I32))

        def one_pass(ps, o, e, h, s, a, first=1):
            g = e * PASSES + a
            c, at = divmod(e * C + s * P, PIECE)
            nc.tensor.matmul_mx(
                out=ps[:, o : o + P],
                lhsT=w_t[:, g, 2 * P * h : 2 * P * (h + 1)].bitcast(FP4X4),
                lhsT_scale=ws_t[:, g, P * h : P * (h + 1)],
                rhs=g_codes[a][c][:, at : at + P].bitcast(FP8X4),
                rhs_scale=(g_scales, g_scales1)[a][c][:, at : at + P],
                start=(a == first),
                stop=(a != first),
            )

        def half(e, h):
            ps = psum.tile([P, C], F32, name="ps")
            for s in range(2):
                for a in (1, 0):
                    one_pass(ps, s * P, e, h, s, a)
            nc.scalar.activation(y[h][:, e * C : (e + 1) * C], ps[:], RELU, bias=b_t[:, h, e : e + 1])

        def expert(e):
            for h in range(HALVES):
                half(e, h)

        def words(a, lo, n):
            gather_codes(a, lo, lo + n)

        for c in range(3):
            words(0, PIECE * c, PIECE)
        for c in range(len(CHUNKS[1])):
            quantize(1, c)
        gather_scales(0)
        gather_scales(1)
        words(1, 0, PIECE)
        for e in range(3):
            expert(e)
        gather_scales(2)
        words(1, PIECE, PIECE)
        for e in range(3, 6):
            expert(e)
        gather_scales(3)
        words(1, 2 * PIECE, PIECE)
        for e in range(6, 9):
            half(e, 0)
        words(0, 3 * PIECE, PIECE)
        ends = []
        for s in range(2):
            ps = psum.tile([P, C], F32, name="ps")
            one_pass(ps, 0, E - 1, 0, s, 0, first=0)
            ends.append(ps)
        for e in range(9, E - 1):
            words(1, e * C, C)
            half(e, 0)
        words(1, (E - 1) * C, C)
        for s in range(2):
            one_pass(ends[s], 0, E - 1, 0, s, 1, first=0)
            at = (E - 1) * C + s * P
            nc.scalar.activation(y[0][:, at : at + P], ends[s][:, 0:P], RELU, bias=b_t[:, 0, E - 1 : E])
        for e in range(6, E):
            half(e, 1)

        gate_t = []
        for r, a in enumerate((1, 1, 0)):
            gate_t.append(gathered[a].tile([P, T], F32, align_bytes=64, name=f"g_codes{a}"))
            nc.sync.dma_start(out=gate_t[r][:], in_=gate[r, 0:P, :])

        def product(h, r, lo, hi):
            prod = work.tile([P, hi - lo], F32, name=f"prod{r}_{hi - lo}")
            nc.vector.tensor_tensor(prod[:], y[h][:].indirect(pos_t[r][:, lo // 16 : hi // 16]), gate_t[r][:, lo:hi], MULT)
            return prod

        def add(into, other):
            nc.vector.tensor_tensor(into[:], into[:], other[:], ADD)

        def store(h, lo, hi, total):
            nc.sync.dma_start(out=out[h * P : (h + 1) * P, lo:hi], in_=total[:])

        a0 = product(0, 0, 0, T)
        a1 = product(0, 1, 0, T)
        a2 = product(0, 2, 0, T)
        add(a0, a1)
        b0 = product(1, 0, 0, CUT)
        add(a0, a2)
        store(0, 0, T, a0)
        b1 = product(1, 1, 0, CUT)
        b2 = product(1, 2, 0, CUT)
        add(b0, b1)
        c0 = product(1, 0, CUT, T)
        add(b0, b2)
        store(1, 0, CUT, b0)
        c1 = product(1, 1, CUT, T)
        c2 = product(1, 2, CUT, T)
        add(c0, c1)
        add(c0, c2)
        store(1, CUT, T, c0)
